import numpy as np
import ml_dtypes


def mxq(x, axis, fmt="e4m3"):
    dtype, down = {"e4m3": (ml_dtypes.float8_e4m3fn, 7), "e5m2": (ml_dtypes.float8_e5m2, 14)}[fmt]
    v = np.moveaxis(np.asarray(x, np.float32).astype(ml_dtypes.bfloat16).astype(np.float64), axis, -1)
    blocks = v.reshape(v.shape[:-1] + (-1, 32))
    amax = np.abs(blocks).max(-1, keepdims=True)
    byte = np.maximum(np.where(amax > 0, np.frexp(amax)[1] - 1 + 127, 0) - down, 1)
    scale = np.exp2(byte - 127.0)
    codes = (blocks / scale).astype(np.float32).astype(dtype).astype(np.float64)
    return np.moveaxis((codes * scale).reshape(v.shape), -1, axis)


WIDE = False


def mx_kscale(k):
    if not WIDE:
        return np.ones(k)
    levels = np.array([10, -10, 5, -5, 0])
    if k % 512:
        return np.exp2(np.random.permutation(np.resize(levels, k // 32))).repeat(32)
    a = np.empty((k // 512, 16))
    for p in range(k // 512):
        a[p, :8] = np.random.permutation(np.resize(levels, 8))
        for g in range(8):
            far = levels[np.abs(levels - a[p, g]) >= 10]
            a[p, g + 8] = far[np.random.randint(len(far))]
    return np.exp2(a.ravel()).repeat(32)


def f64(x):
    return np.asarray(x).astype(np.float64)


E2M1 = np.array([0.0, 0.5, 1.0, 1.5, 2.0, 3.0, 4.0, 6.0, -0.0, -0.5, -1.0, -1.5, -2.0, -3.0, -4.0, -6.0])


def pack_weight(w, fmt):
    k, n = w.shape
    w = f64(np.asarray(w, np.float32).astype(ml_dtypes.bfloat16)).reshape(k // 32, 32, n)
    amax = np.abs(w).max(1)
    if fmt == "e4m3":
        byte = np.frexp(amax)[1] - 1 + 127 - 7
    else:
        mant, ex = np.frexp(amax / 6.0)
        byte = np.where(mant > 0.5, ex, ex - 1) + 127
    byte = np.clip(np.where(amax > 0, byte, 1), 1, 254)
    scaled = (w * np.exp2(127.0 - byte)[:, None, :]).reshape(k, n).astype(np.float32)
    by_word = np.ascontiguousarray(scaled.reshape(k // 512, 128, 4, n).transpose(0, 1, 3, 2))
    if fmt == "e4m3":
        words = by_word.astype(ml_dtypes.float8_e4m3fn).view(np.uint8)
    else:
        c = by_word.astype(ml_dtypes.float4_e2m1fn).view(np.uint8) & 0xF
        words = (c[..., 0::2] | (c[..., 1::2] << 4)).reshape(k // 512, 128, 2 * n)
    return np.ascontiguousarray(words), np.ascontiguousarray(byte.astype(np.uint8).reshape(k // 512, 16, n))


def unpack_weight(words, scales, fmt):
    g, _, n = scales.shape
    words = np.ascontiguousarray(words).reshape(g, 128, n, -1)
    if fmt == "e4m3":
        vals = words.view(ml_dtypes.float8_e4m3fn).astype(np.float64)
    else:
        nib = np.empty((g, 128, n, 4), np.uint8)
        nib[..., 0::2] = words & 0xF
        nib[..., 1::2] = words >> 4
        vals = E2M1[nib]
    vals = vals * np.repeat(np.exp2(scales.astype(np.float64) - 127.0), 8, axis=1)[..., None]
    return vals.transpose(0, 1, 3, 2).reshape(g * 512, n)


K, M, T = 1536, 1536, 1024


def setup_inputs():
    n = np.random.standard_normal
    s = mx_kscale(K)[:, None]
    w = n((K, M)) / np.sqrt(K) / s
    w4 = pack_weight(w, "e2m1")
    rest = w - unpack_weight(*w4, "e2m1")
    p_r8 = pack_weight(rest, "e4m3")
    return {
        "x": (n((K, T)) * s).astype(np.float32),
        "w4_words": w4[0],
        "w4_scales": w4[1],
        "r8_words": p_r8[0],
        "r8_scales": p_r8[1],
    }


def reference(x, w4_words, w4_scales, r8_words, r8_scales):
    x_ = mxq(f64(x), 0, "e4m3")
    w4_ = unpack_weight(w4_words, w4_scales, "e2m1")
    r8_ = unpack_weight(r8_words, r8_scales, "e4m3")
    y = x_.T @ w4_ + x_.T @ r8_
    return np.maximum(y, 0.0) ** 2

@@ -1,0 +1,204 @@
+from contextlib import ExitStack
+
+import concourse.mybir as mybir
+
+K, N, T = 1536, 1536, 1024
+FLOPS = 2 * 2 * K * N * T
+
+F32 = mybir.dt.float32
+BF16 = mybir.dt.bfloat16
+I32 = mybir.dt.int32
+U32 = mybir.dt.uint32
+U8 = mybir.dt.uint8
+E4M3 = mybir.dt.float8_e4m3fn_x4
+E2M1 = mybir.dt.float4_e2m1fn_x4
+MULT = mybir.AluOpType.mult
+RELU = mybir.ActivationFunctionType.Relu
+
+P = 128
+PACK = 4
+PASSES = K // (P * PACK)
+NB = 512
+HALF = T // 2
+TT = HALF // P
+LEFT = 2 * NB
+
+
+def tile_mix_resid_tm_relu2_kernel(tc, x, w4_words, w4_scales, r8_words, r8_scales, out):
+    nc = tc.nc
+    with ExitStack() as ctx:
+        keep = ctx.enter_context(tc.tile_pool(name="keep", bufs=1))
+        relu_pool = ctx.enter_context(tc.tile_pool(name="relu", bufs=4))
+        out_pool = ctx.enter_context(tc.tile_pool(name="outs", bufs=16))
+        psum = ctx.enter_context(tc.psum_pool(name="psum", bufs=8))
+        ctx.enter_context(tc.manual_schedule())
+
+        raw, grouped, codes, xs = {}, {}, {}, {}
+        for a in range(PASSES):
+            for h in range(2):
+                raw[a, h] = keep.tile([P, PACK, HALF], F32, name=f"raw{a}{h}", align_bytes=64)
+                grouped[a, h] = keep.tile([P, HALF, PACK], BF16, name=f"grp{a}{h}", align_bytes=64)
+                codes[a, h] = keep.tile([P, HALF], U32, name=f"cod{a}{h}", align_bytes=64)
+                xs[a, h] = keep.tile([P, HALF], U8, name=f"xs{a}{h}", align_bytes=64)
+        w4_left = [keep.tile([P, 2 * LEFT], U8, name=f"w4l{a}", align_bytes=64) for a in range(PASSES)]
+        r8_left = [keep.tile([P, LEFT], U32, name=f"r8l{a}", align_bytes=64) for a in range(PASSES)]
+        w4_right = keep.tile([P, PASSES, 2 * NB], U8, name="w4r", align_bytes=64)
+        r8_right = keep.tile([P, PASSES, NB], U32, name="r8r", align_bytes=64)
+        w4s_first = keep.tile([P, 1, N], U8, name="w4s_first", align_bytes=64)
+        w4s_rest = keep.tile([P, PASSES - 1, N], U8, name="w4s_rest", align_bytes=64)
+        r8s = keep.tile([P, PASSES, N], U8, name="r8s", align_bytes=64)
+        warm = keep.tile([P, 8], F32, name="warm")
+
+        nc.vector.memset(w4s_first[:].rearrange("p a n -> p (a n)").bitcast(U32), 0)
+        nc.vector.memset(r8s[:].rearrange("p a n -> p (a n)").bitcast(U32), 0)
+        nc.gpsimd.memset(w4s_rest[:].rearrange("p a n -> p (a n)").bitcast(U32), 0)
+        nc.vector.memset(warm[:], 0.0)
+        nc.scalar.activation(out=warm[:, 0:1], in_=warm[:, 1:2], func=RELU)
+
+        def load_x(a, h, c0, c1):
+            src = x[a * P * PACK : (a + 1) * P * PACK, :].rearrange("(p j) t -> p j t", j=PACK)
+            nc.sync.dma_start(out=raw[a, h][:, :, c0:c1], in_=src[:, :, h * HALF + c0 : h * HALF + c1])
+
+        def load_w4_left(a):
+            nc.sync.dma_start(out=w4_left[a][:].bitcast(I32), in_=w4_words[a][:, 0 : 2 * LEFT].bitcast(I32))
+
+        def load_r8_left(a):
+            src = r8_words[a].rearrange("p n i -> p (n i)")[:, 0 : 4 * LEFT]
+            nc.sync.dma_start(out=r8_left[a][:].bitcast(I32), in_=src.bitcast(I32))
+
+        def load_scales(tile, row0, dram, a0, a1):
+            for q in range(4):
+                src = dram[a0:a1, 4 * q : 4 * q + 4, :].rearrange("a r n -> r a n")
+                dst = tile[32 * q + row0 : 32 * q + row0 + 4, :, :]
+                nc.sync.dma_start(out=dst.bitcast(I32), in_=src.bitcast(I32))
+
+        load_x(0, 0, 0, HALF // 2)
+        load_scales(w4s_first, 0, w4_scales, 0, 1)
+        load_w4_left(0)
+        load_x(0, 0, HALF // 2, HALF)
+        load_scales(r8s, 4, r8_scales, 0, PASSES)
+        load_r8_left(0)
+        load_x(1, 0, 0, HALF)
+        load_scales(w4s_rest, 0, w4_scales, 1, PASSES)
+        load_w4_left(1)
+        load_r8_left(1)
+        load_x(2, 0, 0, HALF)
+        load_w4_left(2)
+        load_r8_left(2)
+        nc.sync.dma_start(
+            out=w4_right[:].bitcast(I32),
+            in_=w4_words.rearrange("a p c -> p a c")[:, :, 2 * LEFT : 2 * N].bitcast(I32),
+        )
+        nc.sync.dma_start(
+            out=r8_right[:].bitcast(I32),
+            in_=r8_words.rearrange("a p n i -> p a (n i)")[:, :, 4 * LEFT : 4 * N].bitcast(I32),
+        )
+        for a in range(PASSES):
+            load_x(a, 1, 0, HALF)
+
+        def group(engine_copy, a, h, t0, t1):
+            cols = slice(t0 * P, t1 * P)
+            engine_copy(
+                out=grouped[a, h][:, cols, :].rearrange("p (c i) j -> p c j i", i=4),
+                in_=raw[a, h][:, :, cols].rearrange("p j (c i) -> p c j i", i=4),
+            )
+
+        def quantise(a, h, t0, t1):
+            cols = slice(t0 * P, t1 * P)
+            nc.vector.quantize_mx(
+                out=codes[a, h][:, cols].bitcast(E4M3),
+                scales=xs[a, h][:, cols],
+                in_=grouped[a, h][:, cols, :].rearrange("p c j -> p (c j)"),
+            )
+
+        def convert_half(a, h):
+            group(nc.scalar.copy, a, h, 3, 4)
+            group(nc.vector.tensor_copy, a, h, 0, 2)
+            group(nc.vector.tensor_copy, a, h, 2, 3)
+            quantise(a, h, 0, 2)
+            quantise(a, h, 2, 4)
+
+        def w4_operand(a, n0, n1):
+            if n0 < LEFT:
+                return w4_left[a][:, 2 * n0 : 2 * n1].bitcast(E2M1)
+            return w4_right[:, a, 2 * (n0 - LEFT) : 2 * (n1 - LEFT)].bitcast(E2M1)
+
+        def r8_operand(a, n0, n1):
+            if n0 < LEFT:
+                return r8_left[a][:, n0:n1].bitcast(E4M3)
+            return r8_right[:, a, n0 - LEFT : n1 - LEFT].bitcast(E4M3)
+
+        def w4_pass(acc, a, t, n0, n1):
+            h, cols = t // TT, slice(t % TT * P, (t % TT + 1) * P)
+            scale = w4s_first[:, 0, n0:n1] if a == 0 else w4s_rest[:, a - 1, n0:n1]
+            nc.tensor.matmul_mx(
+                out=acc[:],
+                lhsT=codes[a, h][:, cols].bitcast(E4M3),
+                lhsT_scale=xs[a, h][:, cols],
+                rhs=w4_operand(a, n0, n1),
+                rhs_scale=scale,
+                start=(a == 0),
+                stop=False,
+            )
+
+        def r8_pass(acc, a, t, n0, n1):
+            h, cols = t // TT, slice(t % TT * P, (t % TT + 1) * P)
+            nc.tensor.matmul_mx(
+                out=acc[:],
+                lhsT=codes[a, h][:, cols].bitcast(E4M3),
+                lhsT_scale=xs[a, h][:, cols],
+                rhs=r8_operand(a, n0, n1),
+                rhs_scale=r8s[4:P, a, n0:n1],
+                start=False,
+                stop=(a == PASSES - 1),
+            )
+
+        def finish(acc, t, n0, n1):
+            pos = relu_pool.tile([P, n1 - n0], F32, name="pos")
+            nc.scalar.activation(out=pos[:], in_=acc[:], func=RELU)
+            res = out_pool.tile([P, n1 - n0], F32, name="res")
+            nc.vector.tensor_tensor(out=res[:], in0=pos[:], in1=pos[:], op=MULT)
+            nc.sync.dma_start(out=out[t * P : (t + 1) * P, n0:n1], in_=res[:])
+
+        def block(t, n0, n1):
+            acc = psum.tile([P, n1 - n0], F32, name="acc")
+            for a in range(PASSES):
+                w4_pass(acc, a, t, n0, n1)
+                r8_pass(acc, a, t, n0, n1)
+            return acc
+
+        group(nc.scalar.copy, 0, 0, 1, 2)
+        group(nc.vector.tensor_copy, 0, 0, 0, 1)
+        quantise(0, 0, 0, 1)
+        quantise(0, 0, 1, 2)
+        group(nc.scalar.copy, 0, 0, 3, 4)
+        group(nc.vector.tensor_copy, 0, 0, 2, 3)
+        quantise(0, 0, 2, 3)
+        quantise(0, 0, 3, 4)
+        convert_half(1, 0)
+        convert_half(2, 0)
+        first = [(t, n0) for t in range(TT) for n0 in range(0, LEFT, NB)]
+        accs = [psum.tile([P, NB], F32, name="acc") for i in first]
+        for a in range(PASSES):
+            for acc, (t, n0) in zip(accs, first):
+                w4_pass(acc, a, t, n0, n0 + NB)
+            for acc, (t, n0) in zip(accs, first):
+                r8_pass(acc, a, t, n0, n0 + NB)
+        for acc, (t, n0) in zip(accs, first):
+            finish(acc, t, n0, n0 + NB)
+
+        for t in range(TT):
+            if t < PASSES:
+                convert_half(t, 1)
+            acc = block(t, LEFT, N)
+            finish(acc, t, LEFT, N)
+
+        for t in range(TT, 2 * TT):
+            for n0 in range(0, N, NB):
+                if t == 2 * TT - 1 and n0 == N - NB:
+                    for m0 in range(n0, N, P):
+                        acc = block(t, m0, m0 + P)
+                        finish(acc, t, m0, m0 + P)
+                else:
+                    acc = block(t, n0, n0 + NB)
+                    finish(acc, t, n0, n0 + NB)

@@ -29,7 +29,7 @@ def tile_mix_resid_tm_relu2_kernel(tc, x, w4_words, w4_scales, r8_words, r8_scal
     with ExitStack() as ctx:
         keep = ctx.enter_context(tc.tile_pool(name="keep", bufs=1))
         relu_pool = ctx.enter_context(tc.tile_pool(name="relu", bufs=4))
-        out_pool = ctx.enter_context(tc.tile_pool(name="outs", bufs=16))
+        out_pool = ctx.enter_context(tc.tile_pool(name="outs", bufs=8))
         psum = ctx.enter_context(tc.psum_pool(name="psum", bufs=8))
         ctx.enter_context(tc.manual_schedule())
 
@@ -44,15 +44,17 @@ def tile_mix_resid_tm_relu2_kernel(tc, x, w4_words, w4_scales, r8_words, r8_scal
         r8_left = [keep.tile([P, LEFT], U32, name=f"r8l{a}", align_bytes=64) for a in range(PASSES)]
         w4_right = keep.tile([P, PASSES, 2 * NB], U8, name="w4r", align_bytes=64)
         r8_right = keep.tile([P, PASSES, NB], U32, name="r8r", align_bytes=64)
-        w4s_first = keep.tile([P, 1, N], U8, name="w4s_first", align_bytes=64)
-        w4s_rest = keep.tile([P, PASSES - 1, N], U8, name="w4s_rest", align_bytes=64)
-        r8s = keep.tile([P, PASSES, N], U8, name="r8s", align_bytes=64)
+        w4s_left = keep.tile([P, PASSES, LEFT], U8, name="w4sl", align_bytes=64)
+        r8s_left = keep.tile([P, PASSES, LEFT], U8, name="r8sl", align_bytes=64)
+        w4s_right = keep.tile([P, PASSES, NB], U8, name="w4sr", align_bytes=64)
+        r8s_right = keep.tile([P, PASSES, NB], U8, name="r8sr", align_bytes=64)
         warm = keep.tile([P, 8], F32, name="warm")
 
-        nc.vector.memset(w4s_first[:].rearrange("p a n -> p (a n)").bitcast(U32), 0)
-        nc.vector.memset(r8s[:].rearrange("p a n -> p (a n)").bitcast(U32), 0)
-        nc.gpsimd.memset(w4s_rest[:].rearrange("p a n -> p (a n)").bitcast(U32), 0)
-        nc.vector.memset(warm[:], 0.0)
+        nc.vector.memset(w4s_left[:].rearrange("p a n -> p (a n)").bitcast(U32), 0)
+        nc.vector.memset(r8s_left[:].rearrange("p a n -> p (a n)").bitcast(U32), 0)
+        nc.gpsimd.memset(warm[:], 0.0)
+        nc.gpsimd.memset(w4s_right[:].rearrange("p a n -> p (a n)").bitcast(U32), 0)
+        nc.gpsimd.memset(r8s_right[:].rearrange("p a n -> p (a n)").bitcast(U32), 0)
         nc.scalar.activation(out=warm[:, 0:1], in_=warm[:, 1:2], func=RELU)
 
         def load_x(a, h, c0, c1):
@@ -66,25 +68,26 @@ def tile_mix_resid_tm_relu2_kernel(tc, x, w4_words, w4_scales, r8_words, r8_scal
             src = r8_words[a].rearrange("p n i -> p (n i)")[:, 0 : 4 * LEFT]
             nc.sync.dma_start(out=r8_left[a][:].bitcast(I32), in_=src.bitcast(I32))
 
-        def load_scales(tile, row0, dram, a0, a1):
-            for q in range(4):
-                src = dram[a0:a1, 4 * q : 4 * q + 4, :].rearrange("a r n -> r a n")
-                dst = tile[32 * q + row0 : 32 * q + row0 + 4, :, :]
-                nc.sync.dma_start(out=dst.bitcast(I32), in_=src.bitcast(I32))
+        def load_scales(tile, row0, dram, n0, n1):
+            by_row = dram.rearrange("a (q r) n -> r q a n", r=4)
+            for r in range(4):
+                dst = tile[row0 + r : P : 32, :, :]
+                nc.sync.dma_start(out=dst.bitcast(I32), in_=by_row[r, :, :, n0:n1].bitcast(I32))
 
         load_x(0, 0, 0, HALF // 2)
-        load_scales(w4s_first, 0, w4_scales, 0, 1)
+        load_scales(w4s_left, 0, w4_scales, 0, LEFT)
         load_w4_left(0)
         load_x(0, 0, HALF // 2, HALF)
-        load_scales(r8s, 4, r8_scales, 0, PASSES)
         load_r8_left(0)
+        load_scales(r8s_left, 4, r8_scales, 0, LEFT)
         load_x(1, 0, 0, HALF)
-        load_scales(w4s_rest, 0, w4_scales, 1, PASSES)
         load_w4_left(1)
         load_r8_left(1)
         load_x(2, 0, 0, HALF)
         load_w4_left(2)
         load_r8_left(2)
+        load_scales(w4s_right, 0, w4_scales, LEFT, N)
+        load_scales(r8s_right, 4, r8_scales, LEFT, N)
         nc.sync.dma_start(
             out=w4_right[:].bitcast(I32),
             in_=w4_words.rearrange("a p c -> p a c")[:, :, 2 * LEFT : 2 * N].bitcast(I32),
@@ -96,15 +99,15 @@ def tile_mix_resid_tm_relu2_kernel(tc, x, w4_words, w4_scales, r8_words, r8_scal
         for a in range(PASSES):
             load_x(a, 1, 0, HALF)
 
-        def group(engine_copy, a, h, t0, t1):
-            cols = slice(t0 * P, t1 * P)
+        def group(engine_copy, a, h, t):
+            cols = slice(t * P, (t + 1) * P)
             engine_copy(
                 out=grouped[a, h][:, cols, :].rearrange("p (c i) j -> p c j i", i=4),
                 in_=raw[a, h][:, :, cols].rearrange("p j (c i) -> p c j i", i=4),
             )
 
-        def quantise(a, h, t0, t1):
-            cols = slice(t0 * P, t1 * P)
+        def quantise(a, h, t):
+            cols = slice(t * P, (t + 1) * P)
             nc.vector.quantize_mx(
                 out=codes[a, h][:, cols].bitcast(E4M3),
                 scales=xs[a, h][:, cols],
@@ -112,93 +115,92 @@ def tile_mix_resid_tm_relu2_kernel(tc, x, w4_words, w4_scales, r8_words, r8_scal
             )
 
         def convert_half(a, h):
-            group(nc.scalar.copy, a, h, 3, 4)
-            group(nc.vector.tensor_copy, a, h, 0, 2)
-            group(nc.vector.tensor_copy, a, h, 2, 3)
-            quantise(a, h, 0, 2)
-            quantise(a, h, 2, 4)
+            group(nc.scalar.copy, a, h, 1)
+            group(nc.scalar.copy, a, h, 3)
+            group(nc.vector.tensor_copy, a, h, 0)
+            quantise(a, h, 0)
+            group(nc.vector.tensor_copy, a, h, 2)
+            quantise(a, h, 1)
+            quantise(a, h, 2)
+            quantise(a, h, 3)
 
-        def w4_operand(a, n0, n1):
-            if n0 < LEFT:
-                return w4_left[a][:, 2 * n0 : 2 * n1].bitcast(E2M1)
-            return w4_right[:, a, 2 * (n0 - LEFT) : 2 * (n1 - LEFT)].bitcast(E2M1)
-
-        def r8_operand(a, n0, n1):
-            if n0 < LEFT:
-                return r8_left[a][:, n0:n1].bitcast(E4M3)
-            return r8_right[:, a, n0 - LEFT : n1 - LEFT].bitcast(E4M3)
-
-        def w4_pass(acc, a, t, n0, n1):
+        def x_operand(a, t):
             h, cols = t // TT, slice(t % TT * P, (t % TT + 1) * P)
-            scale = w4s_first[:, 0, n0:n1] if a == 0 else w4s_rest[:, a - 1, n0:n1]
-            nc.tensor.matmul_mx(
-                out=acc[:],
-                lhsT=codes[a, h][:, cols].bitcast(E4M3),
-                lhsT_scale=xs[a, h][:, cols],
-                rhs=w4_operand(a, n0, n1),
-                rhs_scale=scale,
-                start=(a == 0),
-                stop=False,
-            )
+            return codes[a, h][:, cols].bitcast(E4M3), xs[a, h][:, cols]
 
-        def r8_pass(acc, a, t, n0, n1):
-            h, cols = t // TT, slice(t % TT * P, (t % TT + 1) * P)
-            nc.tensor.matmul_mx(
-                out=acc[:],
-                lhsT=codes[a, h][:, cols].bitcast(E4M3),
-                lhsT_scale=xs[a, h][:, cols],
-                rhs=r8_operand(a, n0, n1),
-                rhs_scale=r8s[4:P, a, n0:n1],
-                start=False,
-                stop=(a == PASSES - 1),
-            )
+        def w4_pass(acc, a, t, n0, n1, start, stop):
+            if n0 < LEFT:
+                words, scale = w4_left[a][:, 2 * n0 : 2 * n1], w4s_left[:, a, n0:n1]
+            else:
+                m0, m1 = n0 - LEFT, n1 - LEFT
+                words, scale = w4_right[:, a, 2 * m0 : 2 * m1], w4s_right[:, a, m0:m1]
+            lhs, lhs_scale = x_operand(a, t)
+            nc.tensor.matmul_mx(out=acc[:], lhsT=lhs, lhsT_scale=lhs_scale, rhs=words.bitcast(E2M1), rhs_scale=scale, start=start, stop=stop)
 
-        def finish(acc, t, n0, n1):
-            pos = relu_pool.tile([P, n1 - n0], F32, name="pos")
+        def r8_pass(acc, a, t, n0, n1, start, stop):
+            if n0 < LEFT:
+                words, scale = r8_left[a][:, n0:n1], r8s_left[4:P, a, n0:n1]
+            else:
+                m0, m1 = n0 - LEFT, n1 - LEFT
+                words, scale = r8_right[:, a, m0:m1], r8s_right[4:P, a, m0:m1]
+            lhs, lhs_scale = x_operand(a, t)
+            nc.tensor.matmul_mx(out=acc[:], lhsT=lhs, lhsT_scale=lhs_scale, rhs=words.bitcast(E4M3), rhs_scale=scale, start=start, stop=stop)
+
+        def finish(acc, res):
+            pos = relu_pool.tile([P, acc.shape[1]], F32, name="pos")
             nc.scalar.activation(out=pos[:], in_=acc[:], func=RELU)
-            res = out_pool.tile([P, n1 - n0], F32, name="res")
-            nc.vector.tensor_tensor(out=res[:], in0=pos[:], in1=pos[:], op=MULT)
+            nc.vector.tensor_tensor(out=res, in0=pos[:], in1=pos[:], op=MULT)
+
+        def store(res, t, n0, n1):
             nc.sync.dma_start(out=out[t * P : (t + 1) * P, n0:n1], in_=res[:])
 
-        def block(t, n0, n1):
-            acc = psum.tile([P, n1 - n0], F32, name="acc")
-            for a in range(PASSES):
-                w4_pass(acc, a, t, n0, n1)
-                r8_pass(acc, a, t, n0, n1)
-            return acc
+        LAST = PASSES - 1
 
-        group(nc.scalar.copy, 0, 0, 1, 2)
-        group(nc.vector.tensor_copy, 0, 0, 0, 1)
-        quantise(0, 0, 0, 1)
-        quantise(0, 0, 1, 2)
-        group(nc.scalar.copy, 0, 0, 3, 4)
-        group(nc.vector.tensor_copy, 0, 0, 2, 3)
-        quantise(0, 0, 2, 3)
-        quantise(0, 0, 3, 4)
+        def sweep(tokens, pairwise):
+            work = [(t, n0) for t in tokens for n0 in range(0, LEFT, NB)]
+            accs = [psum.tile([P, NB], F32, name="acc") for i in work]
+            for a in range(PASSES):
+                for acc, (t, n0) in zip(accs, work):
+                    w4_pass(acc, a, t, n0, n0 + NB, a == 0, False)
+                    if pairwise:
+                        r8_pass(acc, a, t, n0, n0 + NB, False, a == LAST)
+                if not pairwise:
+                    for acc, (t, n0) in zip(accs, work):
+                        r8_pass(acc, a, t, n0, n0 + NB, False, a == LAST)
+            for i, t in enumerate(tokens):
+                res = out_pool.tile([P, LEFT], F32, name="wide")
+                finish(accs[2 * i], res[:, 0:NB])
+                finish(accs[2 * i + 1], res[:, NB:LEFT])
+                store(res, t, 0, LEFT)
+
+        convert_half(0, 0)
         convert_half(1, 0)
         convert_half(2, 0)
-        first = [(t, n0) for t in range(TT) for n0 in range(0, LEFT, NB)]
-        accs = [psum.tile([P, NB], F32, name="acc") for i in first]
-        for a in range(PASSES):
-            for acc, (t, n0) in zip(accs, first):
-                w4_pass(acc, a, t, n0, n0 + NB)
-            for acc, (t, n0) in zip(accs, first):
-                r8_pass(acc, a, t, n0, n0 + NB)
-        for acc, (t, n0) in zip(accs, first):
-            finish(acc, t, n0, n0 + NB)
+        sweep(range(TT), False)
 
+        accs = [psum.tile([P, NB], F32, name="acc") for t in range(TT)]
+        for a in range(PASSES):
+            for t in range(TT):
+                w4_pass(accs[t], a, t, LEFT, N, a == 0, False)
+        for t in range(TT):
+            for a in range(PASSES):
+                r8_pass(accs[t], a, t, LEFT, N, False, a == LAST)
         for t in range(TT):
             if t < PASSES:
                 convert_half(t, 1)
-            acc = block(t, LEFT, N)
-            finish(acc, t, LEFT, N)
+            res = out_pool.tile([P, NB], F32, name="narrow")
+            finish(accs[t], res[:])
+            store(res, t, LEFT, N)
+
+        sweep(range(TT, 2 * TT), True)
 
         for t in range(TT, 2 * TT):
-            for n0 in range(0, N, NB):
-                if t == 2 * TT - 1 and n0 == N - NB:
-                    for m0 in range(n0, N, P):
-                        acc = block(t, m0, m0 + P)
-                        finish(acc, t, m0, m0 + P)
-                else:
-                    acc = block(t, n0, n0 + NB)
-                    finish(acc, t, n0, n0 + NB)
+            width = P if t == 2 * TT - 1 else NB
+            for n0 in range(LEFT, N, width):
+                acc = psum.tile([P, width], F32, name="acc")
+                for a in range(PASSES):
+                    w4_pass(acc, a, t, n0, n0 + width, a == 0, False)
+                    r8_pass(acc, a, t, n0, n0 + width, False, a == LAST)
+                res = out_pool.tile([P, width], F32, name="narrow")
+                finish(acc, res[:])
+                store(res, t, n0, n0 + width)

@@ -1,6 +1,7 @@
 from contextlib import ExitStack
 
 import concourse.mybir as mybir
+from concourse.masks import make_identity
 
 K, N, T = 1536, 1536, 1024
 FLOPS = 2 * 2 * K * N * T
@@ -22,6 +23,7 @@ NB = 512
 HALF = T // 2
 TT = HALF // P
 LEFT = 2 * NB
+WARM_TRANSPOSES = 24
 
 
 def tile_mix_resid_tm_relu2_kernel(tc, x, w4_words, w4_scales, r8_words, r8_scales, out):
@@ -36,23 +38,25 @@ def tile_mix_resid_tm_relu2_kernel(tc, x, w4_words, w4_scales, r8_words, r8_scal
         raw, grouped, codes, xs = {}, {}, {}, {}
         for a in range(PASSES):
             for h in range(2):
-                raw[a, h] = keep.tile([P, PACK, HALF], F32, name=f"raw{a}{h}", align_bytes=64)
-                grouped[a, h] = keep.tile([P, HALF, PACK], BF16, name=f"grp{a}{h}", align_bytes=64)
-                codes[a, h] = keep.tile([P, HALF], U32, name=f"cod{a}{h}", align_bytes=64)
-                xs[a, h] = keep.tile([P, HALF], U8, name=f"xs{a}{h}", align_bytes=64)
-        w4_left = [keep.tile([P, 2 * LEFT], U8, name=f"w4l{a}", align_bytes=64) for a in range(PASSES)]
-        r8_left = [keep.tile([P, LEFT], U32, name=f"r8l{a}", align_bytes=64) for a in range(PASSES)]
-        w4_right = keep.tile([P, PASSES, 2 * NB], U8, name="w4r", align_bytes=64)
-        r8_right = keep.tile([P, PASSES, NB], U32, name="r8r", align_bytes=64)
-        w4s_left = keep.tile([P, PASSES, LEFT], U8, name="w4sl", align_bytes=64)
-        r8s_left = keep.tile([P, PASSES, LEFT], U8, name="r8sl", align_bytes=64)
-        w4s_right = keep.tile([P, PASSES, NB], U8, name="w4sr", align_bytes=64)
-        r8s_right = keep.tile([P, PASSES, NB], U8, name="r8sr", align_bytes=64)
+                raw[a, h] = keep.tile([P, PACK, HALF], F32, name=f"raw{a}{h}", align_bytes=256)
+                grouped[a, h] = keep.tile([P, HALF, PACK], BF16, name=f"grp{a}{h}", align_bytes=256)
+                codes[a, h] = keep.tile([P, HALF], U32, name=f"cod{a}{h}", align_bytes=256)
+                xs[a, h] = keep.tile([P, TT, 2 * P], U8, name=f"xs{a}{h}", align_bytes=256)
+        w4_left = [keep.tile([P, 2 * LEFT], U8, name=f"w4l{a}", align_bytes=256) for a in range(PASSES)]
+        r8_left = [keep.tile([P, LEFT], U32, name=f"r8l{a}", align_bytes=256) for a in range(PASSES)]
+        w4_right = keep.tile([P, PASSES, 2 * NB], U8, name="w4r", align_bytes=256)
+        r8_right = keep.tile([P, PASSES, NB], U32, name="r8r", align_bytes=256)
+        w4s_left = keep.tile([P, PASSES, LEFT], U8, name="w4sl", align_bytes=256)
+        r8s_left = keep.tile([P, PASSES, LEFT], U8, name="r8sl", align_bytes=256)
+        w4s_right = keep.tile([P, PASSES, NB], U8, name="w4sr", align_bytes=256)
+        r8s_right = keep.tile([P, PASSES, NB], U8, name="r8sr", align_bytes=256)
         warm = keep.tile([P, 8], F32, name="warm")
 
         nc.vector.memset(w4s_left[:].rearrange("p a n -> p (a n)").bitcast(U32), 0)
         nc.vector.memset(r8s_left[:].rearrange("p a n -> p (a n)").bitcast(U32), 0)
         nc.gpsimd.memset(warm[:], 0.0)
+        ident = keep.tile([P, P], BF16, name="ident")
+        make_identity(nc, ident[:])
         nc.gpsimd.memset(w4s_right[:].rearrange("p a n -> p (a n)").bitcast(U32), 0)
         nc.gpsimd.memset(r8s_right[:].rearrange("p a n -> p (a n)").bitcast(U32), 0)
         nc.scalar.activation(out=warm[:, 0:1], in_=warm[:, 1:2], func=RELU)
@@ -110,7 +114,7 @@ def tile_mix_resid_tm_relu2_kernel(tc, x, w4_words, w4_scales, r8_words, r8_scal
             cols = slice(t * P, (t + 1) * P)
             nc.vector.quantize_mx(
                 out=codes[a, h][:, cols].bitcast(E4M3),
-                scales=xs[a, h][:, cols],
+                scales=xs[a, h][:, t, 0:P],
                 in_=grouped[a, h][:, cols, :].rearrange("p c j -> p (c j)"),
             )
 
@@ -126,7 +130,7 @@ def tile_mix_resid_tm_relu2_kernel(tc, x, w4_words, w4_scales, r8_words, r8_scal
 
         def x_operand(a, t):
             h, cols = t // TT, slice(t % TT * P, (t % TT + 1) * P)
-            return codes[a, h][:, cols].bitcast(E4M3), xs[a, h][:, cols]
+            return codes[a, h][:, cols].bitcast(E4M3), xs[a, h][:, t % TT, 0:P]
 
         def w4_pass(acc, a, t, n0, n1, start, stop):
             if n0 < LEFT:
@@ -173,6 +177,10 @@ def tile_mix_resid_tm_relu2_kernel(tc, x, w4_words, w4_scales, r8_words, r8_scal
                 finish(accs[2 * i + 1], res[:, NB:LEFT])
                 store(res, t, 0, LEFT)
 
+        idle = psum.tile([P, 4, P], BF16, name="acc")
+        for i in range(WARM_TRANSPOSES):
+            nc.tensor.transpose(idle[:, i % 4, :], ident[:], ident[:])
+
         convert_half(0, 0)
         convert_half(1, 0)
         convert_half(2, 0)
@@ -185,12 +193,13 @@ def tile_mix_resid_tm_relu2_kernel(tc, x, w4_words, w4_scales, r8_words, r8_scal
         for t in range(TT):
             for a in range(PASSES):
                 r8_pass(accs[t], a, t, LEFT, N, False, a == LAST)
+        convert_half(0, 1)
         for t in range(TT):
-            if t < PASSES:
-                convert_half(t, 1)
             res = out_pool.tile([P, NB], F32, name="narrow")
             finish(accs[t], res[:])
             store(res, t, LEFT, N)
+            if t % 2 == 1:
+                convert_half(t // 2 + 1, 1)
 
         sweep(range(TT, 2 * TT), True)
 

from contextlib import ExitStack

import concourse.mybir as mybir
from concourse.masks import make_identity

K, N, T = 1536, 1536, 1024
FLOPS = 2 * 2 * K * N * T

F32 = mybir.dt.float32
BF16 = mybir.dt.bfloat16
I32 = mybir.dt.int32
U32 = mybir.dt.uint32
U8 = mybir.dt.uint8
E4M3 = mybir.dt.float8_e4m3fn_x4
E2M1 = mybir.dt.float4_e2m1fn_x4
MULT = mybir.AluOpType.mult
RELU = mybir.ActivationFunctionType.Relu

P = 128
PACK = 4
PASSES = K // (P * PACK)
NB = 512
HALF = T // 2
TT = HALF // P
LEFT = 2 * NB
WARM_TRANSPOSES = 24


def tile_mix_resid_tm_relu2_kernel(tc, x, w4_words, w4_scales, r8_words, r8_scales, out):
    nc = tc.nc
    with ExitStack() as ctx:
        keep = ctx.enter_context(tc.tile_pool(name="keep", bufs=1))
        relu_pool = ctx.enter_context(tc.tile_pool(name="relu", bufs=4))
        out_pool = ctx.enter_context(tc.tile_pool(name="outs", bufs=8))
        psum = ctx.enter_context(tc.psum_pool(name="psum", bufs=8))
        ctx.enter_context(tc.manual_schedule())

        raw, grouped, codes, xs = {}, {}, {}, {}
        for a in range(PASSES):
            for h in range(2):
                raw[a, h] = keep.tile([P, PACK, HALF], F32, name=f"raw{a}{h}", align_bytes=256)
                grouped[a, h] = keep.tile([P, HALF, PACK], BF16, name=f"grp{a}{h}", align_bytes=256)
                codes[a, h] = keep.tile([P, HALF], U32, name=f"cod{a}{h}", align_bytes=256)
                xs[a, h] = keep.tile([P, TT, 2 * P], U8, name=f"xs{a}{h}", align_bytes=256)
        w4_left = [keep.tile([P, 2 * LEFT], U8, name=f"w4l{a}", align_bytes=256) for a in range(PASSES)]
        r8_left = [keep.tile([P, LEFT], U32, name=f"r8l{a}", align_bytes=256) for a in range(PASSES)]
        w4_right = keep.tile([P, PASSES, 2 * NB], U8, name="w4r", align_bytes=256)
        r8_right = keep.tile([P, PASSES, NB], U32, name="r8r", align_bytes=256)
        w4s_left = keep.tile([P, PASSES, LEFT], U8, name="w4sl", align_bytes=256)
        r8s_left = keep.tile([P, PASSES, LEFT], U8, name="r8sl", align_bytes=256)
        w4s_right = keep.tile([P, PASSES, NB], U8, name="w4sr", align_bytes=256)
        r8s_right = keep.tile([P, PASSES, NB], U8, name="r8sr", align_bytes=256)
        warm = keep.tile([P, 8], F32, name="warm")

        nc.vector.memset(w4s_left[:].rearrange("p a n -> p (a n)").bitcast(U32), 0)
        nc.vector.memset(r8s_left[:].rearrange("p a n -> p (a n)").bitcast(U32), 0)
        nc.gpsimd.memset(warm[:], 0.0)
        ident = keep.tile([P, P], BF16, name="ident")
        make_identity(nc, ident[:])
        nc.gpsimd.memset(w4s_right[:].rearrange("p a n -> p (a n)").bitcast(U32), 0)
        nc.gpsimd.memset(r8s_right[:].rearrange("p a n -> p (a n)").bitcast(U32), 0)
        nc.scalar.activation(out=warm[:, 0:1], in_=warm[:, 1:2], func=RELU)

        def load_x(a, h, c0, c1):
            src = x[a * P * PACK : (a + 1) * P * PACK, :].rearrange("(p j) t -> p j t", j=PACK)
            nc.sync.dma_start(out=raw[a, h][:, :, c0:c1], in_=src[:, :, h * HALF + c0 : h * HALF + c1])

        def load_w4_left(a):
            nc.sync.dma_start(out=w4_left[a][:].bitcast(I32), in_=w4_words[a][:, 0 : 2 * LEFT].bitcast(I32))

        def load_r8_left(a):
            src = r8_words[a].rearrange("p n i -> p (n i)")[:, 0 : 4 * LEFT]
            nc.sync.dma_start(out=r8_left[a][:].bitcast(I32), in_=src.bitcast(I32))

        def load_scales(tile, row0, dram, n0, n1):
            by_row = dram.rearrange("a (q r) n -> r q a n", r=4)
            for r in range(4):
                dst = tile[row0 + r : P : 32, :, :]
                nc.sync.dma_start(out=dst.bitcast(I32), in_=by_row[r, :, :, n0:n1].bitcast(I32))

        load_x(0, 0, 0, HALF // 2)
        load_scales(w4s_left, 0, w4_scales, 0, LEFT)
        load_w4_left(0)
        load_x(0, 0, HALF // 2, HALF)
        load_r8_left(0)
        load_scales(r8s_left, 4, r8_scales, 0, LEFT)
        load_x(1, 0, 0, HALF)
        load_w4_left(1)
        load_r8_left(1)
        load_x(2, 0, 0, HALF)
        load_w4_left(2)
        load_r8_left(2)
        load_scales(w4s_right, 0, w4_scales, LEFT, N)
        load_scales(r8s_right, 4, r8_scales, LEFT, N)
        nc.sync.dma_start(
            out=w4_right[:].bitcast(I32),
            in_=w4_words.rearrange("a p c -> p a c")[:, :, 2 * LEFT : 2 * N].bitcast(I32),
        )
        nc.sync.dma_start(
            out=r8_right[:].bitcast(I32),
            in_=r8_words.rearrange("a p n i -> p a (n i)")[:, :, 4 * LEFT : 4 * N].bitcast(I32),
        )
        for a in range(PASSES):
            load_x(a, 1, 0, HALF)

        def group(engine_copy, a, h, t):
            cols = slice(t * P, (t + 1) * P)
            engine_copy(
                out=grouped[a, h][:, cols, :].rearrange("p (c i) j -> p c j i", i=4),
                in_=raw[a, h][:, :, cols].rearrange("p j (c i) -> p c j i", i=4),
            )

        def quantise(a, h, t):
            cols = slice(t * P, (t + 1) * P)
            nc.vector.quantize_mx(
                out=codes[a, h][:, cols].bitcast(E4M3),
                scales=xs[a, h][:, t, 0:P],
                in_=grouped[a, h][:, cols, :].rearrange("p c j -> p (c j)"),
            )

        def convert_half(a, h):
            group(nc.scalar.copy, a, h, 1)
            group(nc.scalar.copy, a, h, 3)
            group(nc.vector.tensor_copy, a, h, 0)
            quantise(a, h, 0)
            group(nc.vector.tensor_copy, a, h, 2)
            quantise(a, h, 1)
            quantise(a, h, 2)
            quantise(a, h, 3)

        def x_operand(a, t):
            h, cols = t // TT, slice(t % TT * P, (t % TT + 1) * P)
            return codes[a, h][:, cols].bitcast(E4M3), xs[a, h][:, t % TT, 0:P]

        def w4_pass(acc, a, t, n0, n1, start, stop):
            if n0 < LEFT:
                words, scale = w4_left[a][:, 2 * n0 : 2 * n1], w4s_left[:, a, n0:n1]
            else:
                m0, m1 = n0 - LEFT, n1 - LEFT
                words, scale = w4_right[:, a, 2 * m0 : 2 * m1], w4s_right[:, a, m0:m1]
            lhs, lhs_scale = x_operand(a, t)
            nc.tensor.matmul_mx(out=acc[:], lhsT=lhs, lhsT_scale=lhs_scale, rhs=words.bitcast(E2M1), rhs_scale=scale, start=start, stop=stop)

        def r8_pass(acc, a, t, n0, n1, start, stop):
            if n0 < LEFT:
                words, scale = r8_left[a][:, n0:n1], r8s_left[4:P, a, n0:n1]
            else:
                m0, m1 = n0 - LEFT, n1 - LEFT
                words, scale = r8_right[:, a, m0:m1], r8s_right[4:P, a, m0:m1]
            lhs, lhs_scale = x_operand(a, t)
            nc.tensor.matmul_mx(out=acc[:], lhsT=lhs, lhsT_scale=lhs_scale, rhs=words.bitcast(E4M3), rhs_scale=scale, start=start, stop=stop)

        def finish(acc, res):
            pos = relu_pool.tile([P, acc.shape[1]], F32, name="pos")
            nc.scalar.activation(out=pos[:], in_=acc[:], func=RELU)
            nc.vector.tensor_tensor(out=res, in0=pos[:], in1=pos[:], op=MULT)

        def store(res, t, n0, n1):
            nc.sync.dma_start(out=out[t * P : (t + 1) * P, n0:n1], in_=res[:])

        LAST = PASSES - 1

        def sweep(tokens, pairwise):
            work = [(t, n0) for t in tokens for n0 in range(0, LEFT, NB)]
            accs = [psum.tile([P, NB], F32, name="acc") for i in work]
            for a in range(PASSES):
                for acc, (t, n0) in zip(accs, work):
                    w4_pass(acc, a, t, n0, n0 + NB, a == 0, False)
                    if pairwise:
                        r8_pass(acc, a, t, n0, n0 + NB, False, a == LAST)
                if not pairwise:
                    for acc, (t, n0) in zip(accs, work):
                        r8_pass(acc, a, t, n0, n0 + NB, False, a == LAST)
            for i, t in enumerate(tokens):
                res = out_pool.tile([P, LEFT], F32, name="wide")
                finish(accs[2 * i], res[:, 0:NB])
                finish(accs[2 * i + 1], res[:, NB:LEFT])
                store(res, t, 0, LEFT)

        idle = psum.tile([P, 4, P], BF16, name="acc")
        for i in range(WARM_TRANSPOSES):
            nc.tensor.transpose(idle[:, i % 4, :], ident[:], ident[:])

        convert_half(0, 0)
        convert_half(1, 0)
        convert_half(2, 0)
        sweep(range(TT), False)

        accs = [psum.tile([P, NB], F32, name="acc") for t in range(TT)]
        for a in range(PASSES):
            for t in range(TT):
                w4_pass(accs[t], a, t, LEFT, N, a == 0, False)
        for t in range(TT):
            for a in range(PASSES):
                r8_pass(accs[t], a, t, LEFT, N, False, a == LAST)
        convert_half(0, 1)
        for t in range(TT):
            res = out_pool.tile([P, NB], F32, name="narrow")
            finish(accs[t], res[:])
            store(res, t, LEFT, N)
            if t % 2 == 1:
                convert_half(t // 2 + 1, 1)

        sweep(range(TT, 2 * TT), True)

        for t in range(TT, 2 * TT):
            width = P if t == 2 * TT - 1 else NB
            for n0 in range(LEFT, N, width):
                acc = psum.tile([P, width], F32, name="acc")
                for a in range(PASSES):
                    w4_pass(acc, a, t, n0, n0 + width, a == 0, False)
                    r8_pass(acc, a, t, n0, n0 + width, False, a == LAST)
                res = out_pool.tile([P, width], F32, name="narrow")
                finish(acc, res[:])
                store(res, t, n0, n0 + width)
